import numpy as np
import ml_dtypes


def mxq(x, axis, fmt="e4m3"):
    dtype, down = {"e4m3": (ml_dtypes.float8_e4m3fn, 7), "e5m2": (ml_dtypes.float8_e5m2, 14)}[fmt]
    v = np.moveaxis(np.asarray(x, np.float32).astype(ml_dtypes.bfloat16).astype(np.float64), axis, -1)
    blocks = v.reshape(v.shape[:-1] + (-1, 32))
    amax = np.abs(blocks).max(-1, keepdims=True)
    byte = np.maximum(np.where(amax > 0, np.frexp(amax)[1] - 1 + 127, 0) - down, 1)
    scale = np.exp2(byte - 127.0)
    codes = (blocks / scale).astype(np.float32).astype(dtype).astype(np.float64)
    return np.moveaxis((codes * scale).reshape(v.shape), -1, axis)


WIDE = False


def mx_kscale(k):
    if not WIDE:
        return np.ones(k)
    levels = np.array([10, -10, 5, -5, 0])
    if k % 512:
        return np.exp2(np.random.permutation(np.resize(levels, k // 32))).repeat(32)
    a = np.empty((k // 512, 16))
    for p in range(k // 512):
        a[p, :8] = np.random.permutation(np.resize(levels, 8))
        for g in range(8):
            far = levels[np.abs(levels - a[p, g]) >= 10]
            a[p, g + 8] = far[np.random.randint(len(far))]
    return np.exp2(a.ravel()).repeat(32)


def f64(x):
    return np.asarray(x).astype(np.float64)


def striped(idx):
    return np.tile(idx.reshape(-1, 16).T, (8, 1)).astype(np.uint16)


def unstriped(offs):
    return offs[:16].T.reshape(-1).astype(np.int64)


def striped8(idx):
    return np.concatenate([x.reshape(-1, 16).T for x in idx]).astype(np.uint16)


def runs(offs, k):
    lists = np.stack([offs[16 * r : 16 * r + 16].T.reshape(-1) for r in range(8)]).astype(np.int64)
    return lists[np.arange(k) % 512 // 64]


def pack_weight(w):
    k, n = w.shape
    w = f64(np.asarray(w, np.float32).astype(ml_dtypes.bfloat16)).reshape(k // 32, 32, n)
    amax = np.abs(w).max(1)
    byte = np.clip(np.where(amax > 0, np.frexp(amax)[1] - 1 + 127 - 7, 1), 1, 254)
    scaled = (w * np.exp2(127.0 - byte)[:, None, :]).reshape(k, n).astype(np.float32)
    words = np.ascontiguousarray(scaled.reshape(k // 512, 128, 4, n).transpose(0, 1, 3, 2)).astype(ml_dtypes.float8_e4m3fn).view(np.uint8)
    return words, np.ascontiguousarray(byte.astype(np.uint8).reshape(k // 512, 16, n))


def unpack_weight(words, scales):
    g, p, n, _ = words.shape
    vals = np.ascontiguousarray(words).view(ml_dtypes.float8_e4m3fn).astype(np.float64) * np.repeat(np.exp2(scales.astype(np.float64) - 127.0), 8, axis=1)[..., None]
    return vals.transpose(0, 1, 3, 2).reshape(g * 512, n)


K, T, S, G, H, C = 512, 1024, 512, 2048, 512, 512


def setup_inputs():
    n = np.random.standard_normal
    s = mx_kscale(K)[:, None]
    packed_xT = pack_weight(n((K, T)) * s)
    packed_dT = pack_weight(n((K, G)) / s)
    return {
        "x_words": packed_xT[0],
        "x_scales": packed_xT[1],
        "d_words": packed_dT[0],
        "d_scales": packed_dT[1],
        "gs": (np.random.uniform(0.5, 1.5, (K, 1)) / s).astype(np.float32),
        "offs": striped(np.random.permutation(T)[:S]),
        "k1": striped8(np.random.randint(0, G, (8, H))),
        "n1": striped8(np.stack([np.random.permutation(S) for _ in range(8)])),
        "n2": striped8(np.stack([np.random.permutation(S) for _ in range(8)])),
        "cand": striped(np.random.permutation(T)[:C]),
        "n3": striped8(np.stack([np.random.permutation(S) for _ in range(8)])),
        "n4": striped8(np.stack([np.random.permutation(S) for _ in range(8)])),
    }


def reference(x_words, x_scales, d_words, d_scales, gs, offs, k1, n1, n2, cand, n3, n4):
    x_cand = unpack_weight(x_words, x_scales)[:, unstriped(cand)]
    d_k1 = unpack_weight(d_words, d_scales)[np.arange(K)[:, None], runs(k1, K)]
    xq = unpack_weight(x_words, x_scales)[:, unstriped(offs)]
    h = 0.0625 * (d_k1.T @ xq)
    z = f64(gs) * ((h[np.arange(H)[:, None], runs(n1, H)]) / (np.abs(h) + np.abs(h[np.arange(H)[:, None], runs(n2, H)]) + 0.5))
    s = 0.0625 * ((x_cand.T @ mxq(z, 0, "e4m3")))
    return s[np.arange(C)[:, None], runs(n3, C)] - (s[np.arange(C)[:, None], runs(n4, C)])

@@ -1,0 +1,221 @@
+from contextlib import ExitStack
+
+import concourse.mybir as mybir
+from concourse.masks import make_identity
+
+F32 = mybir.dt.float32
+BF16 = mybir.dt.bfloat16
+U32 = mybir.dt.uint32
+I32 = mybir.dt.int32
+U16 = mybir.dt.uint16
+U8 = mybir.dt.uint8
+FP8X4 = mybir.dt.float8_e4m3fn_x4
+ACT = mybir.ActivationFunctionType
+ALU = mybir.AluOpType
+
+P = 128
+PACK = 4
+T, G, N = 1024, 2048, 512
+HALF = N // 2
+FLOPS = 2 * 2 * 512 * 512 * 512
+
+
+def tile_picked_pqcnorm2gap_none_p_kernel(
+    tc, x_words, x_scales, d_words, d_scales, gs, offs, k1, n1, n2, cand, n3, n4, out
+):
+    nc = tc.nc
+    with ExitStack() as ctx:
+        keep = ctx.enter_context(tc.tile_pool(name="keep", bufs=1))
+        psum = ctx.enter_context(tc.psum_pool(name="psum", bufs=1))
+
+        def load_list(src, name):
+            tile = keep.tile([P, N // 16], U16, name=name)
+            nc.sync.dma_start(tile[:], src)
+            return tile
+
+        def load_scale_rows(src, width, name):
+            tile = keep.tile([P, width], U8, name=name)
+            rows = src[0].bitcast(I32)
+            nc.sync.dma_start(tile[:].bitcast(I32), rows.unsqueeze(1).to_broadcast([16, 8, width // 4]))
+            return tile
+
+        def load_words(src, width, name):
+            tile = keep.tile([P, width], U32, name=name)
+            nc.sync.dma_start(tile[:].bitcast(I32), src[0].rearrange("p n t -> p (n t)").bitcast(I32))
+            return tile
+
+        def entries(tile, lo, hi):
+            return tile[:, lo // 16 : hi // 16]
+
+        one = keep.tile([P, 1], F32)
+        warm = keep.tile([P, 1], F32)
+        nc.gpsimd.memset(one[:], 1.0)
+        nc.scalar.activation(warm[:], one[:], ACT.Abs_reciprocal_sqrt)
+
+        k1_l = load_list(k1, "k1_l")
+        d_rows = load_scale_rows(d_scales, G, "d_rows")
+        offs_l = load_list(offs, "offs_l")
+        x_rows = load_scale_rows(x_scales, T, "x_rows")
+        cand_l = load_list(cand, "cand_l")
+        n2_l = load_list(n2, "n2_l")
+        n1_l = load_list(n1, "n1_l")
+        d_table = load_words(d_words, G, "d_table")
+        x_table = load_words(x_words, T, "x_table")
+        n4_l = load_list(n4, "n4_l")
+        n3_l = load_list(n3, "n3_l")
+        gain = keep.tile([P, PACK], F32)
+        nc.gpsimd.dma_start(gain[:], gs.rearrange("(p t) o -> p (t o)", t=PACK))
+
+        size = [keep.tile([P, 2 * N], F32, name="size%d" % t) for t in range(PACK)]
+        for t in range(PACK):
+            nc.vector.memset(size[t][:, N:], 0.0)
+        planes = keep.tile([P, 2 * N], U8, align_bytes=64)
+        nc.gpsimd.memset(planes[:].bitcast(U32), 0)
+        c_plane = keep.tile([P, N], U8, align_bytes=64)
+        nc.gpsimd.memset(c_plane[:].bitcast(U32), 0)
+        ident = keep.tile([P, P], F32)
+        make_identity(nc, ident[:])
+
+        def move_rows(dst, src):
+            for r in range(4):
+                queue = nc.sync if r % 2 == 0 else nc.scalar
+                queue.dma_start(dst[:].bitcast(I32)[r:P:32, :], src[:].bitcast(I32)[8 * r : P : 32, :])
+
+        def deal_scales(dst, src):
+            nc.vector.tensor_copy(dst.rearrange("p (t m) -> p t m", t=PACK), src.rearrange("p (m t) -> p t m", t=PACK))
+
+        d_bytes = keep.tile([P, N], U8, align_bytes=64)
+        xq_bytes = keep.tile([P, N], U8, align_bytes=64)
+        c_bytes = keep.tile([P, N], U8, align_bytes=64)
+        staged = keep.tile([P, 2 * N], U8, align_bytes=64)
+        c_staged = keep.tile([P, N], U8, align_bytes=64)
+        nc.vector.tensor_copy(d_bytes[:], d_rows[:].indirect(k1_l[:]))
+        nc.vector.tensor_copy(xq_bytes[:], x_rows[:].indirect(offs_l[:]))
+        deal_scales(staged[:, N:], d_bytes[:])
+        nc.vector.tensor_copy(staged[:, 0:N].bitcast(I32), xq_bytes[:].bitcast(I32))
+        move_rows(planes, staged)
+        nc.vector.tensor_copy(c_bytes[:], x_rows[:].indirect(cand_l[:]))
+        deal_scales(c_staged[:], c_bytes[:])
+        move_rows(c_plane, c_staged)
+        xq_plane, d_plane = planes[:, 0:N], planes[:, N:]
+
+        def deal_words(src, name):
+            dealt = keep.tile([P, N], U32, name=name, align_bytes=64)
+            nc.vector.tensor_copy(
+                dealt[:].rearrange("p (t m) -> p m t", t=PACK), src[:].rearrange("p (m t) -> p m t", t=PACK)
+            )
+            return dealt
+
+        d_picked = keep.tile([P, N], U32, align_bytes=64)
+        nc.vector.tensor_copy(d_picked[:], d_table[:].indirect(k1_l[:]))
+        xq_codes = keep.tile([P, N], U32, align_bytes=64)
+        nc.vector.tensor_copy(xq_codes[:], x_table[:].indirect(offs_l[:]))
+        d_codes = deal_words(d_picked, "d_codes")
+
+        banks = [psum.tile([P, N], F32, name="bank%d" % t) for t in range(PACK)]
+        for t in range(PACK):
+            cols = slice(t * P, (t + 1) * P)
+            nc.tensor.matmul_mx(
+                out=banks[t][:],
+                lhsT=d_codes[:, cols].bitcast(FP8X4),
+                lhsT_scale=d_plane[:, cols],
+                rhs=xq_codes[:].bitcast(FP8X4),
+                rhs_scale=xq_plane,
+                start=True,
+                stop=True,
+            )
+
+        c_picked = keep.tile([P, N], U32, align_bytes=64)
+        nc.vector.tensor_copy(c_picked[:], x_table[:].indirect(cand_l[:]))
+        c_codes = deal_words(c_picked, "c_codes")
+
+        def add_by_transposes(a, b):
+            turned = psum.tile([P, N], F32, tag="turned", bufs=2)
+            for lo in range(0, N, P):
+                cols = slice(lo, lo + P)
+                nc.tensor.matmul(turned[:, cols], a[:, cols], ident[:], start=True, stop=False, is_transpose=True)
+                nc.tensor.matmul(turned[:, cols], b[:, cols], ident[:], start=False, stop=True, is_transpose=True)
+            return turned
+
+        def turn_back(a):
+            back = psum.tile([P, N], F32, tag="back", bufs=2)
+            for lo in range(0, N, P):
+                cols = slice(lo, lo + P)
+                nc.tensor.transpose(back[:, cols], a[:, cols], ident[:])
+            return back
+
+        gained = [keep.tile([P, 2 * N], F32, name="gained%d" % t) for t in range(PACK)]
+        inv = keep.tile([P, PACK, N], F32)
+        top = keep.tile([P, PACK, N], F32)
+        for t in range(PACK):
+            nc.scalar.activation(size[t][:, :N], banks[t][:], ACT.Abs, scale=0.0625)
+        for t in range(PACK):
+            other = gained[t][:, N:]
+            nc.vector.tensor_copy(other, size[t][:].indirect(n2_l[:]))
+            turned = add_by_transposes(size[t][:, :N], other)
+            nc.scalar.activation(gained[t][:, :N], banks[t][:], ACT.Copy, scale=gain[:, t : t + 1])
+            root = keep.tile([P, N], F32, name="root%d" % t)
+            nc.scalar.activation(root[:], turned[:], ACT.Abs_reciprocal_sqrt, bias=0.5)
+            back = turn_back(root[:])
+            nc.scalar.activation(inv[:, t, :], back[:], ACT.Square, scale=0.25)
+        for t in range(PACK):
+            nc.vector.tensor_copy(top[:, t, :], gained[t][:].indirect(n1_l[:]))
+
+        score = size
+        banks2 = [psum.tile([P, N], F32, name="bank%d" % t) for t in range(PACK)]
+        chunks = [(0, 256), (256, 512)]
+        zs = []
+        for lo, hi in chunks:
+            z = keep.tile([P, hi - lo, PACK], BF16, name="z%d" % lo, align_bytes=64)
+            nc.vector.tensor_tensor(
+                z[:].rearrange("p (c i) t -> p c t i", i=2),
+                top[:, :, lo:hi].rearrange("p t (c i) -> p c t i", i=2),
+                inv[:, :, lo:hi].rearrange("p t (c i) -> p c t i", i=2),
+                ALU.mult,
+            )
+            zs.append(z)
+        for (lo, hi), z in zip(chunks, zs):
+            cols = slice(lo, hi)
+            z_codes = keep.tile([P, hi - lo], U32, name="z_codes%d" % lo, align_bytes=64)
+            z_plane = keep.tile([P, hi - lo], U8, name="z_plane%d" % lo, align_bytes=64)
+            nc.vector.quantize_mx(
+                out=z_codes[:].bitcast(FP8X4), scales=z_plane[:], in_=z[:].rearrange("p c t -> p (c t)")
+            )
+            for t in range(PACK):
+                rows = slice(t * P, (t + 1) * P)
+                nc.tensor.matmul_mx(
+                    out=banks2[t][:, cols],
+                    lhsT=c_codes[:, rows].bitcast(FP8X4),
+                    lhsT_scale=c_plane[:, rows],
+                    rhs=z_codes[:].bitcast(FP8X4),
+                    rhs_scale=z_plane[:],
+                    start=True,
+                    stop=True,
+                )
+                if t == 0:
+                    nc.scalar.activation(score[t][:, cols], banks2[t][:, cols], ACT.Copy, scale=0.0625)
+        for t in range(1, PACK):
+            nc.scalar.activation(score[t][:, :N], banks2[t][:], ACT.Copy, scale=0.0625)
+
+        out_rows = out.rearrange("(p t) j -> p t j", t=PACK)
+        for t in range(PACK):
+            less = keep.tile([P, N], F32, name="less%d" % t)
+            gap = keep.tile([P, N], F32, name="gap%d" % t)
+            if t < 0:
+                more = keep.tile([P, N], F32, name="more%d" % t)
+                nc.vector.tensor_scalar(less[:], score[t][:].indirect(n4_l[:]), -1.0, 0.0, ALU.mult, ALU.add)
+                nc.vector.tensor_copy(more[:], score[t][:].indirect(n3_l[:]))
+                turned = add_by_transposes(more[:], less[:])
+                flipped = keep.tile([P, N], F32, name="flipped%d" % t)
+                nc.scalar.copy(flipped[:], turned[:])
+                back = turn_back(flipped[:])
+                nc.scalar.copy(gap[:], back[:])
+                nc.sync.dma_start(out_rows[:, t, :], gap[:])
+            else:
+                nc.vector.tensor_copy(less[:], score[t][:].indirect(n4_l[:]))
+                pieces = [(0, 256), (256, 512)] if t == PACK - 1 else [(0, N)]
+                for lo, hi in pieces:
+                    nc.vector.tensor_tensor(
+                        gap[:, lo:hi], score[t][:].indirect(entries(n3_l, lo, hi)), less[:, lo:hi], ALU.subtract
+                    )
+                    nc.sync.dma_start(out_rows[:, t, lo:hi], gap[:, lo:hi])

@@ -1,7 +1,6 @@
 from contextlib import ExitStack
 
 import concourse.mybir as mybir
-from concourse.masks import make_identity
 
 F32 = mybir.dt.float32
 BF16 = mybir.dt.bfloat16
@@ -17,6 +16,7 @@ P = 128
 PACK = 4
 T, G, N = 1024, 2048, 512
 HALF = N // 2
+RUN = 8
 FLOPS = 2 * 2 * 512 * 512 * 512
 
 
@@ -52,19 +52,19 @@ def tile_picked_pqcnorm2gap_none_p_kernel(
         nc.gpsimd.memset(one[:], 1.0)
         nc.scalar.activation(warm[:], one[:], ACT.Abs_reciprocal_sqrt)
 
-        k1_l = load_list(k1, "k1_l")
-        d_rows = load_scale_rows(d_scales, G, "d_rows")
         offs_l = load_list(offs, "offs_l")
         x_rows = load_scale_rows(x_scales, T, "x_rows")
+        k1_l = load_list(k1, "k1_l")
+        d_rows = load_scale_rows(d_scales, G, "d_rows")
         cand_l = load_list(cand, "cand_l")
         n2_l = load_list(n2, "n2_l")
         n1_l = load_list(n1, "n1_l")
         d_table = load_words(d_words, G, "d_table")
         x_table = load_words(x_words, T, "x_table")
+        gain = keep.tile([P, PACK], F32)
+        nc.sync.dma_start(gain[:], gs.rearrange("(p t) o -> p (t o)", t=PACK))
         n4_l = load_list(n4, "n4_l")
         n3_l = load_list(n3, "n3_l")
-        gain = keep.tile([P, PACK], F32)
-        nc.gpsimd.dma_start(gain[:], gs.rearrange("(p t) o -> p (t o)", t=PACK))
 
         size = [keep.tile([P, 2 * N], F32, name="size%d" % t) for t in range(PACK)]
         for t in range(PACK):
@@ -73,8 +73,8 @@ def tile_picked_pqcnorm2gap_none_p_kernel(
         nc.gpsimd.memset(planes[:].bitcast(U32), 0)
         c_plane = keep.tile([P, N], U8, align_bytes=64)
         nc.gpsimd.memset(c_plane[:].bitcast(U32), 0)
-        ident = keep.tile([P, P], F32)
-        make_identity(nc, ident[:])
+        gain16 = keep.tile([P, PACK], F32)
+        nc.gpsimd.tensor_scalar(gain16[:], gain[:], 0.0625, 0.0, ALU.mult, ALU.add)
 
         def move_rows(dst, src):
             for r in range(4):
@@ -86,17 +86,13 @@ def tile_picked_pqcnorm2gap_none_p_kernel(
 
         d_bytes = keep.tile([P, N], U8, align_bytes=64)
         xq_bytes = keep.tile([P, N], U8, align_bytes=64)
-        c_bytes = keep.tile([P, N], U8, align_bytes=64)
         staged = keep.tile([P, 2 * N], U8, align_bytes=64)
         c_staged = keep.tile([P, N], U8, align_bytes=64)
-        nc.vector.tensor_copy(d_bytes[:], d_rows[:].indirect(k1_l[:]))
         nc.vector.tensor_copy(xq_bytes[:], x_rows[:].indirect(offs_l[:]))
-        deal_scales(staged[:, N:], d_bytes[:])
+        nc.vector.tensor_copy(d_bytes[:], d_rows[:].indirect(k1_l[:]))
         nc.vector.tensor_copy(staged[:, 0:N].bitcast(I32), xq_bytes[:].bitcast(I32))
+        deal_scales(staged[:, N:], d_bytes[:])
         move_rows(planes, staged)
-        nc.vector.tensor_copy(c_bytes[:], x_rows[:].indirect(cand_l[:]))
-        deal_scales(c_staged[:], c_bytes[:])
-        move_rows(c_plane, c_staged)
         xq_plane, d_plane = planes[:, 0:N], planes[:, N:]
 
         def deal_words(src, name):
@@ -106,7 +102,7 @@ def tile_picked_pqcnorm2gap_none_p_kernel(
             )
             return dealt
 
-        d_picked = keep.tile([P, N], U32, align_bytes=64)
+        d_picked = keep.tile([P, N], U32, tag="turns", align_bytes=64)
         nc.vector.tensor_copy(d_picked[:], d_table[:].indirect(k1_l[:]))
         xq_codes = keep.tile([P, N], U32, align_bytes=64)
         nc.vector.tensor_copy(xq_codes[:], x_table[:].indirect(offs_l[:]))
@@ -125,41 +121,30 @@ def tile_picked_pqcnorm2gap_none_p_kernel(
                 stop=True,
             )
 
-        c_picked = keep.tile([P, N], U32, align_bytes=64)
-        nc.vector.tensor_copy(c_picked[:], x_table[:].indirect(cand_l[:]))
-        c_codes = deal_words(c_picked, "c_codes")
-
-        def add_by_transposes(a, b):
-            turned = psum.tile([P, N], F32, tag="turned", bufs=2)
-            for lo in range(0, N, P):
-                cols = slice(lo, lo + P)
-                nc.tensor.matmul(turned[:, cols], a[:, cols], ident[:], start=True, stop=False, is_transpose=True)
-                nc.tensor.matmul(turned[:, cols], b[:, cols], ident[:], start=False, stop=True, is_transpose=True)
-            return turned
-
-        def turn_back(a):
-            back = psum.tile([P, N], F32, tag="back", bufs=2)
-            for lo in range(0, N, P):
-                cols = slice(lo, lo + P)
-                nc.tensor.transpose(back[:, cols], a[:, cols], ident[:])
-            return back
+        c_bytes = keep.tile([P, N], U8, tag="turns", align_bytes=64)
+        nc.vector.tensor_copy(c_bytes[:], x_rows[:].indirect(cand_l[:]))
+        c_codes = keep.tile([P, N], U32, align_bytes=64)
+        nc.vector.tensor_copy(
+            c_codes[:].rearrange("p (t g e) -> p g t e", t=PACK, e=RUN), x_table[:].indirect(cand_l[:])
+        )
+        nc.vector.tensor_copy(
+            c_staged[:].bitcast(I32).rearrange("p (t g e) -> p t g e", t=PACK, e=RUN // 4),
+            c_bytes[:].bitcast(I32).rearrange("p (g t e) -> p t g e", t=PACK, e=RUN // 4),
+        )
+        move_rows(c_plane, c_staged)
 
         gained = [keep.tile([P, 2 * N], F32, name="gained%d" % t) for t in range(PACK)]
         inv = keep.tile([P, PACK, N], F32)
         top = keep.tile([P, PACK, N], F32)
+        dens = [keep.tile([P, N], F32, name="den%d" % t) for t in range(PACK)]
         for t in range(PACK):
             nc.scalar.activation(size[t][:, :N], banks[t][:], ACT.Abs, scale=0.0625)
+            nc.scalar.activation(gained[t][:, N:], banks[t][:], ACT.Abs, scale=0.0625)
+            nc.vector.tensor_tensor(dens[t][:], size[t][:].indirect(n2_l[:]), gained[t][:, N:], ALU.add)
         for t in range(PACK):
-            other = gained[t][:, N:]
-            nc.vector.tensor_copy(other, size[t][:].indirect(n2_l[:]))
-            turned = add_by_transposes(size[t][:, :N], other)
-            nc.scalar.activation(gained[t][:, :N], banks[t][:], ACT.Copy, scale=gain[:, t : t + 1])
-            root = keep.tile([P, N], F32, name="root%d" % t)
-            nc.scalar.activation(root[:], turned[:], ACT.Abs_reciprocal_sqrt, bias=0.5)
-            back = turn_back(root[:])
-            nc.scalar.activation(inv[:, t, :], back[:], ACT.Square, scale=0.25)
-        for t in range(PACK):
-            nc.vector.tensor_copy(top[:, t, :], gained[t][:].indirect(n1_l[:]))
+            nc.scalar.activation(gained[t][:, :N], banks[t][:], ACT.Copy, scale=gain16[:, t : t + 1])
+            nc.scalar.activation(inv[:, t, :], dens[t][:], ACT.Abs_reciprocal_sqrt, bias=0.5)
+            nc.vector.tensor_tensor(top[:, t, :], gained[t][:].indirect(n1_l[:]), inv[:, t, :], ALU.mult)
 
         score = size
         banks2 = [psum.tile([P, N], F32, name="bank%d" % t) for t in range(PACK)]
@@ -174,17 +159,19 @@ def tile_picked_pqcnorm2gap_none_p_kernel(
                 ALU.mult,
             )
             zs.append(z)
+        packed = []
         for (lo, hi), z in zip(chunks, zs):
-            cols = slice(lo, hi)
             z_codes = keep.tile([P, hi - lo], U32, name="z_codes%d" % lo, align_bytes=64)
             z_plane = keep.tile([P, hi - lo], U8, name="z_plane%d" % lo, align_bytes=64)
             nc.vector.quantize_mx(
                 out=z_codes[:].bitcast(FP8X4), scales=z_plane[:], in_=z[:].rearrange("p c t -> p (c t)")
             )
-            for t in range(PACK):
-                rows = slice(t * P, (t + 1) * P)
+            packed.append((z_codes, z_plane))
+        for t in range(PACK):
+            rows = slice(t * P, (t + 1) * P)
+            for (lo, hi), (z_codes, z_plane) in zip(chunks, packed):
                 nc.tensor.matmul_mx(
-                    out=banks2[t][:, cols],
+                    out=banks2[t][:, lo:hi],
                     lhsT=c_codes[:, rows].bitcast(FP8X4),
                     lhsT_scale=c_plane[:, rows],
                     rhs=z_codes[:].bitcast(FP8X4),
@@ -193,29 +180,24 @@ def tile_picked_pqcnorm2gap_none_p_kernel(
                     stop=True,
                 )
                 if t == 0:
-                    nc.scalar.activation(score[t][:, cols], banks2[t][:, cols], ACT.Copy, scale=0.0625)
-        for t in range(1, PACK):
-            nc.scalar.activation(score[t][:, :N], banks2[t][:], ACT.Copy, scale=0.0625)
+                    nc.scalar.activation(score[t][:, lo:hi], banks2[t][:, lo:hi], ACT.Copy, scale=0.0625)
+            if t > 0:
+                nc.scalar.activation(score[t][:, :N], banks2[t][:], ACT.Copy, scale=0.0625)
 
-        out_rows = out.rearrange("(p t) j -> p t j", t=PACK)
+        out_rows = out.rearrange("(g t e) j -> t g e j", t=PACK, e=RUN)
         for t in range(PACK):
             less = keep.tile([P, N], F32, name="less%d" % t)
             gap = keep.tile([P, N], F32, name="gap%d" % t)
+            nc.vector.tensor_copy(less[:], score[t][:].indirect(n4_l[:]))
             if t < 0:
                 more = keep.tile([P, N], F32, name="more%d" % t)
-                nc.vector.tensor_scalar(less[:], score[t][:].indirect(n4_l[:]), -1.0, 0.0, ALU.mult, ALU.add)
                 nc.vector.tensor_copy(more[:], score[t][:].indirect(n3_l[:]))
-                turned = add_by_transposes(more[:], less[:])
-                flipped = keep.tile([P, N], F32, name="flipped%d" % t)
-                nc.scalar.copy(flipped[:], turned[:])
-                back = turn_back(flipped[:])
-                nc.scalar.copy(gap[:], back[:])
-                nc.sync.dma_start(out_rows[:, t, :], gap[:])
+                nc.gpsimd.tensor_tensor(gap[:], more[:], less[:], ALU.subtract)
+                nc.sync.dma_start(out_rows[t], gap[:])
             else:
-                nc.vector.tensor_copy(less[:], score[t][:].indirect(n4_l[:]))
                 pieces = [(0, 256), (256, 512)] if t == PACK - 1 else [(0, N)]
                 for lo, hi in pieces:
                     nc.vector.tensor_tensor(
                         gap[:, lo:hi], score[t][:].indirect(entries(n3_l, lo, hi)), less[:, lo:hi], ALU.subtract
                     )
-                    nc.sync.dma_start(out_rows[:, t, lo:hi], gap[:, lo:hi])
+                    nc.sync.dma_start(out_rows[t, :, :, lo:hi], gap[:, lo:hi])

@@ -52,48 +52,40 @@ def tile_picked_pqcnorm2gap_none_p_kernel(
         nc.gpsimd.memset(one[:], 1.0)
         nc.scalar.activation(warm[:], one[:], ACT.Abs_reciprocal_sqrt)
 
-        offs_l = load_list(offs, "offs_l")
-        x_rows = load_scale_rows(x_scales, T, "x_rows")
         k1_l = load_list(k1, "k1_l")
         d_rows = load_scale_rows(d_scales, G, "d_rows")
-        cand_l = load_list(cand, "cand_l")
-        n2_l = load_list(n2, "n2_l")
-        n1_l = load_list(n1, "n1_l")
+        offs_l = load_list(offs, "offs_l")
         d_table = load_words(d_words, G, "d_table")
         x_table = load_words(x_words, T, "x_table")
+        x_rows = keep.tile([P, T], U8)
+        for q in range(4):
+            rows = x_scales[0].bitcast(I32)[4 * q : 4 * q + 4, :]
+            nc.sync.dma_start(
+                x_rows[:].bitcast(I32)[32 * q : 32 * q + 32, :], rows.unsqueeze(0).to_broadcast([8, 4, T // 4])
+            )
+        cand_l = load_list(cand, "cand_l")
         gain = keep.tile([P, PACK], F32)
         nc.sync.dma_start(gain[:], gs.rearrange("(p t) o -> p (t o)", t=PACK))
+        n2_l = load_list(n2, "n2_l")
+        n1_l = load_list(n1, "n1_l")
         n4_l = load_list(n4, "n4_l")
         n3_l = load_list(n3, "n3_l")
 
         size = [keep.tile([P, 2 * N], F32, name="size%d" % t) for t in range(PACK)]
         for t in range(PACK):
             nc.vector.memset(size[t][:, N:], 0.0)
-        planes = keep.tile([P, 2 * N], U8, align_bytes=64)
-        nc.gpsimd.memset(planes[:].bitcast(U32), 0)
-        c_plane = keep.tile([P, N], U8, align_bytes=64)
-        nc.gpsimd.memset(c_plane[:].bitcast(U32), 0)
-        gain16 = keep.tile([P, PACK], F32)
-        nc.gpsimd.tensor_scalar(gain16[:], gain[:], 0.0625, 0.0, ALU.mult, ALU.add)
-
-        def move_rows(dst, src):
-            for r in range(4):
-                queue = nc.sync if r % 2 == 0 else nc.scalar
-                queue.dma_start(dst[:].bitcast(I32)[r:P:32, :], src[:].bitcast(I32)[8 * r : P : 32, :])
-
-        def deal_scales(dst, src):
-            nc.vector.tensor_copy(dst.rearrange("p (t m) -> p t m", t=PACK), src.rearrange("p (m t) -> p t m", t=PACK))
+        d_plane = keep.tile([P, N], U8, align_bytes=64)
+        nc.gpsimd.memset(d_plane[:].bitcast(U32), 0)
 
         d_bytes = keep.tile([P, N], U8, align_bytes=64)
-        xq_bytes = keep.tile([P, N], U8, align_bytes=64)
-        staged = keep.tile([P, 2 * N], U8, align_bytes=64)
-        c_staged = keep.tile([P, N], U8, align_bytes=64)
-        nc.vector.tensor_copy(xq_bytes[:], x_rows[:].indirect(offs_l[:]))
+        staged = keep.tile([P, N], U8, align_bytes=64)
         nc.vector.tensor_copy(d_bytes[:], d_rows[:].indirect(k1_l[:]))
-        nc.vector.tensor_copy(staged[:, 0:N].bitcast(I32), xq_bytes[:].bitcast(I32))
-        deal_scales(staged[:, N:], d_bytes[:])
-        move_rows(planes, staged)
-        xq_plane, d_plane = planes[:, 0:N], planes[:, N:]
+        nc.vector.tensor_copy(
+            staged[:].rearrange("p (t m) -> p t m", t=PACK), d_bytes[:].rearrange("p (m t) -> p t m", t=PACK)
+        )
+        for r in range(4):
+            queue = nc.sync if r % 2 == 0 else nc.scalar
+            queue.dma_start(d_plane[:].bitcast(I32)[r:P:32, :], staged[:].bitcast(I32)[8 * r : P : 32, :])
 
         def deal_words(src, name):
             dealt = keep.tile([P, N], U32, name=name, align_bytes=64)
@@ -107,6 +99,8 @@ def tile_picked_pqcnorm2gap_none_p_kernel(
         xq_codes = keep.tile([P, N], U32, align_bytes=64)
         nc.vector.tensor_copy(xq_codes[:], x_table[:].indirect(offs_l[:]))
         d_codes = deal_words(d_picked, "d_codes")
+        xq_plane = keep.tile([P, N], U8, align_bytes=64)
+        nc.vector.tensor_copy(xq_plane[:], x_rows[:].indirect(offs_l[:]))
 
         banks = [psum.tile([P, N], F32, name="bank%d" % t) for t in range(PACK)]
         for t in range(PACK):
@@ -116,62 +110,78 @@ def tile_picked_pqcnorm2gap_none_p_kernel(
                 lhsT=d_codes[:, cols].bitcast(FP8X4),
                 lhsT_scale=d_plane[:, cols],
                 rhs=xq_codes[:].bitcast(FP8X4),
-                rhs_scale=xq_plane,
+                rhs_scale=xq_plane[:],
                 start=True,
                 stop=True,
             )
 
         c_bytes = keep.tile([P, N], U8, tag="turns", align_bytes=64)
         nc.vector.tensor_copy(c_bytes[:], x_rows[:].indirect(cand_l[:]))
+        c_plane = keep.tile([P, N], U8, align_bytes=64)
         c_codes = keep.tile([P, N], U32, align_bytes=64)
         nc.vector.tensor_copy(
             c_codes[:].rearrange("p (t g e) -> p g t e", t=PACK, e=RUN), x_table[:].indirect(cand_l[:])
         )
         nc.vector.tensor_copy(
-            c_staged[:].bitcast(I32).rearrange("p (t g e) -> p t g e", t=PACK, e=RUN // 4),
+            c_plane[:].bitcast(I32).rearrange("p (t g e) -> p t g e", t=PACK, e=RUN // 4),
             c_bytes[:].bitcast(I32).rearrange("p (g t e) -> p t g e", t=PACK, e=RUN // 4),
         )
-        move_rows(c_plane, c_staged)
 
         gained = [keep.tile([P, 2 * N], F32, name="gained%d" % t) for t in range(PACK)]
-        inv = keep.tile([P, PACK, N], F32)
         top = keep.tile([P, PACK, N], F32)
         dens = [keep.tile([P, N], F32, name="den%d" % t) for t in range(PACK)]
+        on_vector = (2,)
         for t in range(PACK):
             nc.scalar.activation(size[t][:, :N], banks[t][:], ACT.Abs, scale=0.0625)
-            nc.scalar.activation(gained[t][:, N:], banks[t][:], ACT.Abs, scale=0.0625)
-            nc.vector.tensor_tensor(dens[t][:], size[t][:].indirect(n2_l[:]), gained[t][:, N:], ALU.add)
+            if t in (0, 1):
+                nc.gpsimd.tensor_scalar(gained[t][:, N:], size[t][:, :N], 1.0, 0.0, ALU.mult, ALU.add)
+            elif t in on_vector:
+                nc.vector.tensor_copy(gained[t][:, N:], size[t][:, :N])
+            else:
+                nc.scalar.activation(gained[t][:, N:], banks[t][:], ACT.Abs, scale=0.0625)
         for t in range(PACK):
-            nc.scalar.activation(gained[t][:, :N], banks[t][:], ACT.Copy, scale=gain16[:, t : t + 1])
-            nc.scalar.activation(inv[:, t, :], dens[t][:], ACT.Abs_reciprocal_sqrt, bias=0.5)
-            nc.vector.tensor_tensor(top[:, t, :], gained[t][:].indirect(n1_l[:]), inv[:, t, :], ALU.mult)
+            nc.vector.tensor_tensor(dens[t][:], size[t][:].indirect(n2_l[:]), gained[t][:, N:], ALU.add)
+        invs = []
+        for t in range(PACK):
+            nc.scalar.activation(gained[t][:, :N], banks[t][:], ACT.Copy, scale=gain[:, t : t + 1])
+            root = keep.tile([P, N], F32, name="root%d" % t)
+            inv = keep.tile([P, N], F32, name="inv%d" % t)
+            for lo, hi in [(0, HALF), (HALF, N)] if t == PACK - 1 else [(0, N)]:
+                nc.scalar.activation(root[:, lo:hi], dens[t][:, lo:hi], ACT.Abs_reciprocal_sqrt, bias=0.5)
+                nc.scalar.activation(inv[:, lo:hi], root[:, lo:hi], ACT.Square, scale=0.25)
+            invs.append(inv)
+        steps = [(0, 0, N), (1, 0, N), (2, 0, HALF), (3, 0, HALF), (2, HALF, N), (3, HALF, N)]
+        for t, lo, hi in steps:
+            nc.vector.tensor_tensor(
+                top[:, t, lo:hi], gained[t][:].indirect(entries(n1_l, lo, hi)), invs[t][:, lo:hi], ALU.mult
+            )
 
         score = size
-        banks2 = [psum.tile([P, N], F32, name="bank%d" % t) for t in range(PACK)]
-        chunks = [(0, 256), (256, 512)]
+        chunks = [(0, 256, nc.scalar.copy), (256, 384, nc.scalar.copy), (384, 512, nc.vector.tensor_copy)]
         zs = []
-        for lo, hi in chunks:
+        for lo, hi, cast in chunks:
             z = keep.tile([P, hi - lo, PACK], BF16, name="z%d" % lo, align_bytes=64)
-            nc.vector.tensor_tensor(
-                z[:].rearrange("p (c i) t -> p c t i", i=2),
-                top[:, :, lo:hi].rearrange("p t (c i) -> p c t i", i=2),
-                inv[:, :, lo:hi].rearrange("p t (c i) -> p c t i", i=2),
-                ALU.mult,
+            cast(
+                z[:].rearrange("p (c i) t -> p c t i", i=4),
+                top[:, :, lo:hi].rearrange("p t (c i) -> p c t i", i=4),
             )
             zs.append(z)
         packed = []
-        for (lo, hi), z in zip(chunks, zs):
+        for (lo, hi, cast), z in zip(chunks, zs):
             z_codes = keep.tile([P, hi - lo], U32, name="z_codes%d" % lo, align_bytes=64)
             z_plane = keep.tile([P, hi - lo], U8, name="z_plane%d" % lo, align_bytes=64)
             nc.vector.quantize_mx(
                 out=z_codes[:].bitcast(FP8X4), scales=z_plane[:], in_=z[:].rearrange("p c t -> p (c t)")
             )
-            packed.append((z_codes, z_plane))
+            packed.append((lo, hi, z_codes, z_plane))
+        banks2 = [psum.tile([P, N], F32, name="bank%d" % t) for t in range(PACK)]
+        early = psum.tile([P, N], F32)
         for t in range(PACK):
             rows = slice(t * P, (t + 1) * P)
-            for (lo, hi), (z_codes, z_plane) in zip(chunks, packed):
+            for lo, hi, z_codes, z_plane in packed:
+                bank = early if t == 0 and lo == 0 else banks2[t]
                 nc.tensor.matmul_mx(
-                    out=banks2[t][:, lo:hi],
+                    out=bank[:, lo:hi],
                     lhsT=c_codes[:, rows].bitcast(FP8X4),
                     lhsT_scale=c_plane[:, rows],
                     rhs=z_codes[:].bitcast(FP8X4),
@@ -179,9 +189,10 @@ def tile_picked_pqcnorm2gap_none_p_kernel(
                     start=True,
                     stop=True,
                 )
-                if t == 0:
-                    nc.scalar.activation(score[t][:, lo:hi], banks2[t][:, lo:hi], ACT.Copy, scale=0.0625)
-            if t > 0:
+            if t == 0:
+                nc.scalar.activation(score[t][:, :HALF], early[:, :HALF], ACT.Copy, scale=0.0625)
+                nc.vector.tensor_scalar_mul(score[t][:, HALF:N], banks2[t][:, HALF:], 0.0625)
+            else:
                 nc.scalar.activation(score[t][:, :N], banks2[t][:], ACT.Copy, scale=0.0625)
 
         out_rows = out.rearrange("(g t e) j -> t g e j", t=PACK, e=RUN)

@@ -55,14 +55,14 @@ def tile_picked_pqcnorm2gap_none_p_kernel(
         k1_l = load_list(k1, "k1_l")
         d_rows = load_scale_rows(d_scales, G, "d_rows")
         offs_l = load_list(offs, "offs_l")
-        d_table = load_words(d_words, G, "d_table")
-        x_table = load_words(x_words, T, "x_table")
         x_rows = keep.tile([P, T], U8)
         for q in range(4):
             rows = x_scales[0].bitcast(I32)[4 * q : 4 * q + 4, :]
             nc.sync.dma_start(
                 x_rows[:].bitcast(I32)[32 * q : 32 * q + 32, :], rows.unsqueeze(0).to_broadcast([8, 4, T // 4])
             )
+        x_table = load_words(x_words, T, "x_table")
+        d_table = load_words(d_words, G, "d_table")
         cand_l = load_list(cand, "cand_l")
         gain = keep.tile([P, PACK], F32)
         nc.sync.dma_start(gain[:], gs.rearrange("(p t) o -> p (t o)", t=PACK))
@@ -94,23 +94,25 @@ def tile_picked_pqcnorm2gap_none_p_kernel(
             )
             return dealt
 
-        d_picked = keep.tile([P, N], U32, tag="turns", align_bytes=64)
-        nc.vector.tensor_copy(d_picked[:], d_table[:].indirect(k1_l[:]))
-        xq_codes = keep.tile([P, N], U32, align_bytes=64)
-        nc.vector.tensor_copy(xq_codes[:], x_table[:].indirect(offs_l[:]))
-        d_codes = deal_words(d_picked, "d_codes")
         xq_plane = keep.tile([P, N], U8, align_bytes=64)
         nc.vector.tensor_copy(xq_plane[:], x_rows[:].indirect(offs_l[:]))
+        xq_codes = keep.tile([P, N], U32, align_bytes=64)
+        nc.vector.tensor_copy(xq_codes[:], x_table[:].indirect(offs_l[:]))
+        d_picked = keep.tile([P, N], U32, tag="turns", align_bytes=64)
+        nc.vector.tensor_copy(d_picked[:], d_table[:].indirect(k1_l[:]))
+        d_codes = deal_words(d_picked, "d_codes")
 
         banks = [psum.tile([P, N], F32, name="bank%d" % t) for t in range(PACK)]
-        for t in range(PACK):
+        lead = psum.tile([P, N], F32)
+        parts = [(0, 0, HALF, lead), (0, HALF, N, banks[0])] + [(t, 0, N, banks[t]) for t in range(1, PACK)]
+        for t, lo, hi, bank in parts:
             cols = slice(t * P, (t + 1) * P)
             nc.tensor.matmul_mx(
-                out=banks[t][:],
+                out=bank[:, lo:hi],
                 lhsT=d_codes[:, cols].bitcast(FP8X4),
                 lhsT_scale=d_plane[:, cols],
-                rhs=xq_codes[:].bitcast(FP8X4),
-                rhs_scale=xq_plane[:],
+                rhs=xq_codes[:, lo:hi].bitcast(FP8X4),
+                rhs_scale=xq_plane[:, lo:hi],
                 start=True,
                 stop=True,
             )
@@ -130,20 +132,22 @@ def tile_picked_pqcnorm2gap_none_p_kernel(
         gained = [keep.tile([P, 2 * N], F32, name="gained%d" % t) for t in range(PACK)]
         top = keep.tile([P, PACK, N], F32)
         dens = [keep.tile([P, N], F32, name="den%d" % t) for t in range(PACK)]
-        on_vector = (2,)
-        for t in range(PACK):
-            nc.scalar.activation(size[t][:, :N], banks[t][:], ACT.Abs, scale=0.0625)
-            if t in (0, 1):
-                nc.gpsimd.tensor_scalar(gained[t][:, N:], size[t][:, :N], 1.0, 0.0, ALU.mult, ALU.add)
-            elif t in on_vector:
-                nc.vector.tensor_copy(gained[t][:, N:], size[t][:, :N])
+        for t, lo, hi, bank in parts:
+            nc.scalar.activation(size[t][:, lo:hi], bank[:, lo:hi], ACT.Abs, scale=0.0625)
+            twin = gained[t][:, N + lo : N + hi]
+            if t < 2:
+                nc.gpsimd.tensor_scalar(twin, size[t][:, lo:hi], 1.0, 0.0, ALU.mult, ALU.add)
+            elif t == 2:
+                nc.vector.tensor_copy(twin, size[t][:, lo:hi])
             else:
-                nc.scalar.activation(gained[t][:, N:], banks[t][:], ACT.Abs, scale=0.0625)
+                nc.scalar.activation(twin, bank[:, lo:hi], ACT.Abs, scale=0.0625)
         for t in range(PACK):
             nc.vector.tensor_tensor(dens[t][:], size[t][:].indirect(n2_l[:]), gained[t][:, N:], ALU.add)
         invs = []
         for t in range(PACK):
-            nc.scalar.activation(gained[t][:, :N], banks[t][:], ACT.Copy, scale=gain[:, t : t + 1])
+            for u, lo, hi, bank in parts:
+                if u == t:
+                    nc.scalar.activation(gained[t][:, lo:hi], bank[:, lo:hi], ACT.Copy, scale=gain[:, t : t + 1])
             root = keep.tile([P, N], F32, name="root%d" % t)
             inv = keep.tile([P, N], F32, name="inv%d" % t)
             for lo, hi in [(0, HALF), (HALF, N)] if t == PACK - 1 else [(0, N)]:

@@ -14,9 +14,14 @@ ALU = mybir.AluOpType
 
 P = 128
 PACK = 4
+QUADS = 4
 T, G, N = 1024, 2048, 512
 HALF = N // 2
 RUN = 8
+SIXTEENTH = 0.0625
+WHOLE = [(0, N)]
+HALVES = [(0, HALF), (HALF, N)]
+LAST = PACK - 1
 FLOPS = 2 * 2 * 512 * 512 * 512
 
 
@@ -33,12 +38,6 @@ def tile_picked_pqcnorm2gap_none_p_kernel(
             nc.sync.dma_start(tile[:], src)
             return tile
 
-        def load_scale_rows(src, width, name):
-            tile = keep.tile([P, width], U8, name=name)
-            rows = src[0].bitcast(I32)
-            nc.sync.dma_start(tile[:].bitcast(I32), rows.unsqueeze(1).to_broadcast([16, 8, width // 4]))
-            return tile
-
         def load_words(src, width, name):
             tile = keep.tile([P, width], U32, name=name)
             nc.sync.dma_start(tile[:].bitcast(I32), src[0].rearrange("p n t -> p (n t)").bitcast(I32))
@@ -47,16 +46,25 @@ def tile_picked_pqcnorm2gap_none_p_kernel(
         def entries(tile, lo, hi):
             return tile[:, lo // 16 : hi // 16]
 
-        one = keep.tile([P, 1], F32)
-        warm = keep.tile([P, 1], F32)
-        nc.gpsimd.memset(one[:], 1.0)
-        nc.scalar.activation(warm[:], one[:], ACT.Abs_reciprocal_sqrt)
+        def product(bank, left, left_plane, right, right_plane):
+            nc.tensor.matmul_mx(
+                out=bank,
+                lhsT=left.bitcast(FP8X4),
+                lhsT_scale=left_plane,
+                rhs=right.bitcast(FP8X4),
+                rhs_scale=right_plane,
+                start=True,
+                stop=True,
+            )
 
+        d_rows = keep.tile([P, G], U8)
+        nc.sync.dma_start(
+            d_rows[:].bitcast(I32), d_scales[0].bitcast(I32).unsqueeze(1).to_broadcast([16, 8, G // 4])
+        )
         k1_l = load_list(k1, "k1_l")
-        d_rows = load_scale_rows(d_scales, G, "d_rows")
         offs_l = load_list(offs, "offs_l")
         x_rows = keep.tile([P, T], U8)
-        for q in range(4):
+        for q in range(QUADS):
             rows = x_scales[0].bitcast(I32)[4 * q : 4 * q + 4, :]
             nc.sync.dma_start(
                 x_rows[:].bitcast(I32)[32 * q : 32 * q + 32, :], rows.unsqueeze(0).to_broadcast([8, 4, T // 4])
@@ -71,148 +79,126 @@ def tile_picked_pqcnorm2gap_none_p_kernel(
         n4_l = load_list(n4, "n4_l")
         n3_l = load_list(n3, "n3_l")
 
-        size = [keep.tile([P, 2 * N], F32, name="size%d" % t) for t in range(PACK)]
-        for t in range(PACK):
-            nc.vector.memset(size[t][:, N:], 0.0)
+        window = [keep.tile([P, 2 * N], F32, name="window%d" % t) for t in range(PACK)]
+        for t in range(LAST):
+            nc.vector.memset(window[t][:, N:], 0.0)
+        nc.scalar.activation(window[LAST][:, N:], window[0][:, N:], ACT.Abs_reciprocal_sqrt, bias=1.0)
         d_plane = keep.tile([P, N], U8, align_bytes=64)
         nc.gpsimd.memset(d_plane[:].bitcast(U32), 0)
 
         d_bytes = keep.tile([P, N], U8, align_bytes=64)
-        staged = keep.tile([P, N], U8, align_bytes=64)
+        d_dealt = keep.tile([P, N], U8, align_bytes=64)
         nc.vector.tensor_copy(d_bytes[:], d_rows[:].indirect(k1_l[:]))
         nc.vector.tensor_copy(
-            staged[:].rearrange("p (t m) -> p t m", t=PACK), d_bytes[:].rearrange("p (m t) -> p t m", t=PACK)
+            d_dealt[:].rearrange("p (t m) -> p t m", t=PACK), d_bytes[:].rearrange("p (m t) -> p t m", t=PACK)
         )
         for r in range(4):
             queue = nc.sync if r % 2 == 0 else nc.scalar
-            queue.dma_start(d_plane[:].bitcast(I32)[r:P:32, :], staged[:].bitcast(I32)[8 * r : P : 32, :])
-
-        def deal_words(src, name):
-            dealt = keep.tile([P, N], U32, name=name, align_bytes=64)
-            nc.vector.tensor_copy(
-                dealt[:].rearrange("p (t m) -> p m t", t=PACK), src[:].rearrange("p (m t) -> p m t", t=PACK)
-            )
-            return dealt
+            queue.dma_start(d_plane[:].bitcast(I32)[r:P:32, :], d_dealt[:].bitcast(I32)[8 * r : P : 32, :])
 
         xq_plane = keep.tile([P, N], U8, align_bytes=64)
         nc.vector.tensor_copy(xq_plane[:], x_rows[:].indirect(offs_l[:]))
         xq_codes = keep.tile([P, N], U32, align_bytes=64)
         nc.vector.tensor_copy(xq_codes[:], x_table[:].indirect(offs_l[:]))
-        d_picked = keep.tile([P, N], U32, tag="turns", align_bytes=64)
+        d_picked = keep.tile([P, N], U32, tag="in_turn", align_bytes=64)
         nc.vector.tensor_copy(d_picked[:], d_table[:].indirect(k1_l[:]))
-        d_codes = deal_words(d_picked, "d_codes")
+        d_codes = keep.tile([P, N], U32, align_bytes=64)
+        nc.vector.tensor_copy(
+            d_codes[:].rearrange("p (t m) -> p m t", t=PACK), d_picked[:].rearrange("p (m t) -> p m t", t=PACK)
+        )
 
-        banks = [psum.tile([P, N], F32, name="bank%d" % t) for t in range(PACK)]
-        lead = psum.tile([P, N], F32)
-        parts = [(0, 0, HALF, lead), (0, HALF, N, banks[0])] + [(t, 0, N, banks[t]) for t in range(1, PACK)]
-        for t, lo, hi, bank in parts:
+        h_banks = [psum.tile([P, N], F32, name="bank%d" % t) for t in range(PACK)]
+        h_first = psum.tile([P, N], F32)
+        h_parts = [(0, 0, HALF, h_first), (0, HALF, N, h_banks[0])]
+        h_parts = h_parts + [(t, 0, N, h_banks[t]) for t in range(1, PACK)]
+        for t, lo, hi, bank in h_parts:
             cols = slice(t * P, (t + 1) * P)
-            nc.tensor.matmul_mx(
-                out=bank[:, lo:hi],
-                lhsT=d_codes[:, cols].bitcast(FP8X4),
-                lhsT_scale=d_plane[:, cols],
-                rhs=xq_codes[:, lo:hi].bitcast(FP8X4),
-                rhs_scale=xq_plane[:, lo:hi],
-                start=True,
-                stop=True,
-            )
+            product(bank[:, lo:hi], d_codes[:, cols], d_plane[:, cols], xq_codes[:, lo:hi], xq_plane[:, lo:hi])
 
-        c_bytes = keep.tile([P, N], U8, tag="turns", align_bytes=64)
+        c_bytes = keep.tile([P, N], U8, tag="in_turn", align_bytes=64)
         nc.vector.tensor_copy(c_bytes[:], x_rows[:].indirect(cand_l[:]))
         c_plane = keep.tile([P, N], U8, align_bytes=64)
         c_codes = keep.tile([P, N], U32, align_bytes=64)
         nc.vector.tensor_copy(
-            c_codes[:].rearrange("p (t g e) -> p g t e", t=PACK, e=RUN), x_table[:].indirect(cand_l[:])
+            c_codes[:].rearrange("p (t a e) -> p a t e", t=PACK, e=RUN), x_table[:].indirect(cand_l[:])
         )
         nc.vector.tensor_copy(
-            c_plane[:].bitcast(I32).rearrange("p (t g e) -> p t g e", t=PACK, e=RUN // 4),
-            c_bytes[:].bitcast(I32).rearrange("p (g t e) -> p t g e", t=PACK, e=RUN // 4),
+            c_plane[:].bitcast(I32).rearrange("p (t a e) -> p t a e", t=PACK, e=RUN // 4),
+            c_bytes[:].bitcast(I32).rearrange("p (a t e) -> p t a e", t=PACK, e=RUN // 4),
         )
 
         gained = [keep.tile([P, 2 * N], F32, name="gained%d" % t) for t in range(PACK)]
-        top = keep.tile([P, PACK, N], F32)
-        dens = [keep.tile([P, N], F32, name="den%d" % t) for t in range(PACK)]
-        for t, lo, hi, bank in parts:
-            nc.scalar.activation(size[t][:, lo:hi], bank[:, lo:hi], ACT.Abs, scale=0.0625)
+        z_full = keep.tile([P, PACK, N], F32)
+        sums = [keep.tile([P, N], F32, name="sums%d" % t) for t in range(PACK)]
+        for t, lo, hi, bank in h_parts:
+            nc.scalar.activation(window[t][:, lo:hi], bank[:, lo:hi], ACT.Abs, scale=SIXTEENTH)
             twin = gained[t][:, N + lo : N + hi]
-            if t < 2:
-                nc.gpsimd.tensor_scalar(twin, size[t][:, lo:hi], 1.0, 0.0, ALU.mult, ALU.add)
-            elif t == 2:
-                nc.vector.tensor_copy(twin, size[t][:, lo:hi])
+            if t == LAST:
+                nc.scalar.activation(twin, bank[:, lo:hi], ACT.Abs, scale=SIXTEENTH)
+            elif t == 0:
+                nc.gpsimd.tensor_scalar(twin, window[t][:, lo:hi], 1.0, 0.0, ALU.mult, ALU.add)
             else:
-                nc.scalar.activation(twin, bank[:, lo:hi], ACT.Abs, scale=0.0625)
+                nc.vector.tensor_copy(twin, window[t][:, lo:hi])
         for t in range(PACK):
-            nc.vector.tensor_tensor(dens[t][:], size[t][:].indirect(n2_l[:]), gained[t][:, N:], ALU.add)
-        invs = []
+            nc.vector.tensor_tensor(sums[t][:], window[t][:].indirect(n2_l[:]), gained[t][:, N:], ALU.add)
+        inverse = []
         for t in range(PACK):
-            for u, lo, hi, bank in parts:
-                if u == t:
+            for part_t, lo, hi, bank in h_parts:
+                if part_t == t:
                     nc.scalar.activation(gained[t][:, lo:hi], bank[:, lo:hi], ACT.Copy, scale=gain[:, t : t + 1])
             root = keep.tile([P, N], F32, name="root%d" % t)
-            inv = keep.tile([P, N], F32, name="inv%d" % t)
-            for lo, hi in [(0, HALF), (HALF, N)] if t == PACK - 1 else [(0, N)]:
-                nc.scalar.activation(root[:, lo:hi], dens[t][:, lo:hi], ACT.Abs_reciprocal_sqrt, bias=0.5)
-                nc.scalar.activation(inv[:, lo:hi], root[:, lo:hi], ACT.Square, scale=0.25)
-            invs.append(inv)
-        steps = [(0, 0, N), (1, 0, N), (2, 0, HALF), (3, 0, HALF), (2, HALF, N), (3, HALF, N)]
+            inverse.append(keep.tile([P, N], F32, name="inverse%d" % t))
+            for lo, hi in HALVES if t == LAST else WHOLE:
+                nc.scalar.activation(root[:, lo:hi], sums[t][:, lo:hi], ACT.Abs_reciprocal_sqrt, bias=0.5)
+                nc.scalar.activation(inverse[t][:, lo:hi], root[:, lo:hi], ACT.Square, scale=0.25)
+        steps = [(t, 0, N) for t in (0, 1)] + [(t, lo, hi) for lo, hi in HALVES for t in (2, 3)]
         for t, lo, hi in steps:
             nc.vector.tensor_tensor(
-                top[:, t, lo:hi], gained[t][:].indirect(entries(n1_l, lo, hi)), invs[t][:, lo:hi], ALU.mult
+                z_full[:, t, lo:hi], gained[t][:].indirect(entries(n1_l, lo, hi)), inverse[t][:, lo:hi], ALU.mult
             )
 
-        score = size
-        chunks = [(0, 256, nc.scalar.copy), (256, 384, nc.scalar.copy), (384, 512, nc.vector.tensor_copy)]
-        zs = []
+        chunks = [
+            (0, HALF, nc.scalar.copy),
+            (HALF, HALF + P, nc.scalar.copy),
+            (HALF + P, N, nc.vector.tensor_copy),
+        ]
+        woven = []
         for lo, hi, cast in chunks:
-            z = keep.tile([P, hi - lo, PACK], BF16, name="z%d" % lo, align_bytes=64)
+            z_bf16 = keep.tile([P, hi - lo, PACK], BF16, name="z_bf16_%d" % lo, align_bytes=64)
             cast(
-                z[:].rearrange("p (c i) t -> p c t i", i=4),
-                top[:, :, lo:hi].rearrange("p t (c i) -> p c t i", i=4),
+                z_bf16[:].rearrange("p (c i) t -> p c t i", i=4),
+                z_full[:, :, lo:hi].rearrange("p t (c i) -> p c t i", i=4),
             )
-            zs.append(z)
-        packed = []
-        for (lo, hi, cast), z in zip(chunks, zs):
+            woven.append((lo, hi, z_bf16))
+        z_packed = []
+        for lo, hi, z_bf16 in woven:
             z_codes = keep.tile([P, hi - lo], U32, name="z_codes%d" % lo, align_bytes=64)
             z_plane = keep.tile([P, hi - lo], U8, name="z_plane%d" % lo, align_bytes=64)
             nc.vector.quantize_mx(
-                out=z_codes[:].bitcast(FP8X4), scales=z_plane[:], in_=z[:].rearrange("p c t -> p (c t)")
+                out=z_codes[:].bitcast(FP8X4), scales=z_plane[:], in_=z_bf16[:].rearrange("p c t -> p (c t)")
             )
-            packed.append((lo, hi, z_codes, z_plane))
-        banks2 = [psum.tile([P, N], F32, name="bank%d" % t) for t in range(PACK)]
-        early = psum.tile([P, N], F32)
-        for t in range(PACK):
-            rows = slice(t * P, (t + 1) * P)
-            for lo, hi, z_codes, z_plane in packed:
-                bank = early if t == 0 and lo == 0 else banks2[t]
-                nc.tensor.matmul_mx(
-                    out=bank[:, lo:hi],
-                    lhsT=c_codes[:, rows].bitcast(FP8X4),
-                    lhsT_scale=c_plane[:, rows],
-                    rhs=z_codes[:].bitcast(FP8X4),
-                    rhs_scale=z_plane[:],
-                    start=True,
-                    stop=True,
-                )
-            if t == 0:
-                nc.scalar.activation(score[t][:, :HALF], early[:, :HALF], ACT.Copy, scale=0.0625)
-                nc.vector.tensor_scalar_mul(score[t][:, HALF:N], banks2[t][:, HALF:], 0.0625)
-            else:
-                nc.scalar.activation(score[t][:, :N], banks2[t][:], ACT.Copy, scale=0.0625)
+            z_packed.append((lo, hi, z_codes, z_plane))
 
-        out_rows = out.rearrange("(g t e) j -> t g e j", t=PACK, e=RUN)
+        s_banks = [psum.tile([P, N], F32, name="bank%d" % t) for t in range(PACK)]
+        s_first = psum.tile([P, N], F32)
+        for t in range(PACK):
+            cols = slice(t * P, (t + 1) * P)
+            for lo, hi, z_codes, z_plane in z_packed:
+                bank = s_first if t == 0 and lo == 0 else s_banks[t]
+                product(bank[:, lo:hi], c_codes[:, cols], c_plane[:, cols], z_codes[:], z_plane[:])
+            if t == 0:
+                nc.scalar.activation(window[t][:, :HALF], s_first[:, :HALF], ACT.Copy, scale=SIXTEENTH)
+                nc.vector.tensor_scalar_mul(window[t][:, HALF:N], s_banks[t][:, HALF:], SIXTEENTH)
+            else:
+                nc.scalar.activation(window[t][:, :N], s_banks[t][:], ACT.Copy, scale=SIXTEENTH)
+
+        out_rows = out.rearrange("(a t e) j -> t a e j", t=PACK, e=RUN)
         for t in range(PACK):
             less = keep.tile([P, N], F32, name="less%d" % t)
             gap = keep.tile([P, N], F32, name="gap%d" % t)
-            nc.vector.tensor_copy(less[:], score[t][:].indirect(n4_l[:]))
-            if t < 0:
-                more = keep.tile([P, N], F32, name="more%d" % t)
-                nc.vector.tensor_copy(more[:], score[t][:].indirect(n3_l[:]))
-                nc.gpsimd.tensor_tensor(gap[:], more[:], less[:], ALU.subtract)
-                nc.sync.dma_start(out_rows[t], gap[:])
-            else:
-                pieces = [(0, 256), (256, 512)] if t == PACK - 1 else [(0, N)]
-                for lo, hi in pieces:
-                    nc.vector.tensor_tensor(
-                        gap[:, lo:hi], score[t][:].indirect(entries(n3_l, lo, hi)), less[:, lo:hi], ALU.subtract
-                    )
-                    nc.sync.dma_start(out_rows[t, :, :, lo:hi], gap[:, lo:hi])
+            nc.vector.tensor_copy(less[:], window[t][:].indirect(n4_l[:]))
+            for lo, hi in HALVES if t == LAST else WHOLE:
+                nc.vector.tensor_tensor(
+                    gap[:, lo:hi], window[t][:].indirect(entries(n3_l, lo, hi)), less[:, lo:hi], ALU.subtract
+                )
+                nc.sync.dma_start(out_rows[t, :, :, lo:hi], gap[:, lo:hi])

from contextlib import ExitStack

import concourse.mybir as mybir

F32 = mybir.dt.float32
BF16 = mybir.dt.bfloat16
U32 = mybir.dt.uint32
I32 = mybir.dt.int32
U16 = mybir.dt.uint16
U8 = mybir.dt.uint8
FP8X4 = mybir.dt.float8_e4m3fn_x4
ACT = mybir.ActivationFunctionType
ALU = mybir.AluOpType

P = 128
PACK = 4
QUADS = 4
T, G, N = 1024, 2048, 512
HALF = N // 2
RUN = 8
SIXTEENTH = 0.0625
WHOLE = [(0, N)]
HALVES = [(0, HALF), (HALF, N)]
LAST = PACK - 1
FLOPS = 2 * 2 * 512 * 512 * 512


def tile_picked_pqcnorm2gap_none_p_kernel(
    tc, x_words, x_scales, d_words, d_scales, gs, offs, k1, n1, n2, cand, n3, n4, out
):
    nc = tc.nc
    with ExitStack() as ctx:
        keep = ctx.enter_context(tc.tile_pool(name="keep", bufs=1))
        psum = ctx.enter_context(tc.psum_pool(name="psum", bufs=1))

        def load_list(src, name):
            tile = keep.tile([P, N // 16], U16, name=name)
            nc.sync.dma_start(tile[:], src)
            return tile

        def load_words(src, width, name):
            tile = keep.tile([P, width], U32, name=name)
            nc.sync.dma_start(tile[:].bitcast(I32), src[0].rearrange("p n t -> p (n t)").bitcast(I32))
            return tile

        def entries(tile, lo, hi):
            return tile[:, lo // 16 : hi // 16]

        def product(bank, left, left_plane, right, right_plane):
            nc.tensor.matmul_mx(
                out=bank,
                lhsT=left.bitcast(FP8X4),
                lhsT_scale=left_plane,
                rhs=right.bitcast(FP8X4),
                rhs_scale=right_plane,
                start=True,
                stop=True,
            )

        d_rows = keep.tile([P, G], U8)
        nc.sync.dma_start(
            d_rows[:].bitcast(I32), d_scales[0].bitcast(I32).unsqueeze(1).to_broadcast([16, 8, G // 4])
        )
        k1_l = load_list(k1, "k1_l")
        offs_l = load_list(offs, "offs_l")
        x_rows = keep.tile([P, T], U8)
        for q in range(QUADS):
            rows = x_scales[0].bitcast(I32)[4 * q : 4 * q + 4, :]
            nc.sync.dma_start(
                x_rows[:].bitcast(I32)[32 * q : 32 * q + 32, :], rows.unsqueeze(0).to_broadcast([8, 4, T // 4])
            )
        x_table = load_words(x_words, T, "x_table")
        d_table = load_words(d_words, G, "d_table")
        cand_l = load_list(cand, "cand_l")
        gain = keep.tile([P, PACK], F32)
        nc.sync.dma_start(gain[:], gs.rearrange("(p t) o -> p (t o)", t=PACK))
        n2_l = load_list(n2, "n2_l")
        n1_l = load_list(n1, "n1_l")
        n4_l = load_list(n4, "n4_l")
        n3_l = load_list(n3, "n3_l")

        window = [keep.tile([P, 2 * N], F32, name="window%d" % t) for t in range(PACK)]
        for t in range(LAST):
            nc.vector.memset(window[t][:, N:], 0.0)
        nc.scalar.activation(window[LAST][:, N:], window[0][:, N:], ACT.Abs_reciprocal_sqrt, bias=1.0)
        d_plane = keep.tile([P, N], U8, align_bytes=64)
        nc.gpsimd.memset(d_plane[:].bitcast(U32), 0)

        d_bytes = keep.tile([P, N], U8, align_bytes=64)
        d_dealt = keep.tile([P, N], U8, align_bytes=64)
        nc.vector.tensor_copy(d_bytes[:], d_rows[:].indirect(k1_l[:]))
        nc.vector.tensor_copy(
            d_dealt[:].rearrange("p (t m) -> p t m", t=PACK), d_bytes[:].rearrange("p (m t) -> p t m", t=PACK)
        )
        for r in range(4):
            queue = nc.sync if r % 2 == 0 else nc.scalar
            queue.dma_start(d_plane[:].bitcast(I32)[r:P:32, :], d_dealt[:].bitcast(I32)[8 * r : P : 32, :])

        xq_plane = keep.tile([P, N], U8, align_bytes=64)
        nc.vector.tensor_copy(xq_plane[:], x_rows[:].indirect(offs_l[:]))
        xq_codes = keep.tile([P, N], U32, align_bytes=64)
        nc.vector.tensor_copy(xq_codes[:], x_table[:].indirect(offs_l[:]))
        d_picked = keep.tile([P, N], U32, tag="in_turn", align_bytes=64)
        nc.vector.tensor_copy(d_picked[:], d_table[:].indirect(k1_l[:]))
        d_codes = keep.tile([P, N], U32, align_bytes=64)
        nc.vector.tensor_copy(
            d_codes[:].rearrange("p (t m) -> p m t", t=PACK), d_picked[:].rearrange("p (m t) -> p m t", t=PACK)
        )

        h_banks = [psum.tile([P, N], F32, name="bank%d" % t) for t in range(PACK)]
        h_first = psum.tile([P, N], F32)
        h_parts = [(0, 0, HALF, h_first), (0, HALF, N, h_banks[0])]
        h_parts = h_parts + [(t, 0, N, h_banks[t]) for t in range(1, PACK)]
        for t, lo, hi, bank in h_parts:
            cols = slice(t * P, (t + 1) * P)
            product(bank[:, lo:hi], d_codes[:, cols], d_plane[:, cols], xq_codes[:, lo:hi], xq_plane[:, lo:hi])

        c_bytes = keep.tile([P, N], U8, tag="in_turn", align_bytes=64)
        nc.vector.tensor_copy(c_bytes[:], x_rows[:].indirect(cand_l[:]))
        c_plane = keep.tile([P, N], U8, align_bytes=64)
        c_codes = keep.tile([P, N], U32, align_bytes=64)
        nc.vector.tensor_copy(
            c_codes[:].rearrange("p (t a e) -> p a t e", t=PACK, e=RUN), x_table[:].indirect(cand_l[:])
        )
        nc.vector.tensor_copy(
            c_plane[:].bitcast(I32).rearrange("p (t a e) -> p t a e", t=PACK, e=RUN // 4),
            c_bytes[:].bitcast(I32).rearrange("p (a t e) -> p t a e", t=PACK, e=RUN // 4),
        )

        gained = [keep.tile([P, 2 * N], F32, name="gained%d" % t) for t in range(PACK)]
        z_full = keep.tile([P, PACK, N], F32)
        sums = [keep.tile([P, N], F32, name="sums%d" % t) for t in range(PACK)]
        for t, lo, hi, bank in h_parts:
            nc.scalar.activation(window[t][:, lo:hi], bank[:, lo:hi], ACT.Abs, scale=SIXTEENTH)
            twin = gained[t][:, N + lo : N + hi]
            if t == LAST:
                nc.scalar.activation(twin, bank[:, lo:hi], ACT.Abs, scale=SIXTEENTH)
            elif t == 0:
                nc.gpsimd.tensor_scalar(twin, window[t][:, lo:hi], 1.0, 0.0, ALU.mult, ALU.add)
            else:
                nc.vector.tensor_copy(twin, window[t][:, lo:hi])
        for t in range(PACK):
            nc.vector.tensor_tensor(sums[t][:], window[t][:].indirect(n2_l[:]), gained[t][:, N:], ALU.add)
        inverse = []
        for t in range(PACK):
            for part_t, lo, hi, bank in h_parts:
                if part_t == t:
                    nc.scalar.activation(gained[t][:, lo:hi], bank[:, lo:hi], ACT.Copy, scale=gain[:, t : t + 1])
            root = keep.tile([P, N], F32, name="root%d" % t)
            inverse.append(keep.tile([P, N], F32, name="inverse%d" % t))
            for lo, hi in HALVES if t == LAST else WHOLE:
                nc.scalar.activation(root[:, lo:hi], sums[t][:, lo:hi], ACT.Abs_reciprocal_sqrt, bias=0.5)
                nc.scalar.activation(inverse[t][:, lo:hi], root[:, lo:hi], ACT.Square, scale=0.25)
        steps = [(t, 0, N) for t in (0, 1)] + [(t, lo, hi) for lo, hi in HALVES for t in (2, 3)]
        for t, lo, hi in steps:
            nc.vector.tensor_tensor(
                z_full[:, t, lo:hi], gained[t][:].indirect(entries(n1_l, lo, hi)), inverse[t][:, lo:hi], ALU.mult
            )

        chunks = [
            (0, HALF, nc.scalar.copy),
            (HALF, HALF + P, nc.scalar.copy),
            (HALF + P, N, nc.vector.tensor_copy),
        ]
        woven = []
        for lo, hi, cast in chunks:
            z_bf16 = keep.tile([P, hi - lo, PACK], BF16, name="z_bf16_%d" % lo, align_bytes=64)
            cast(
                z_bf16[:].rearrange("p (c i) t -> p c t i", i=4),
                z_full[:, :, lo:hi].rearrange("p t (c i) -> p c t i", i=4),
            )
            woven.append((lo, hi, z_bf16))
        z_packed = []
        for lo, hi, z_bf16 in woven:
            z_codes = keep.tile([P, hi - lo], U32, name="z_codes%d" % lo, align_bytes=64)
            z_plane = keep.tile([P, hi - lo], U8, name="z_plane%d" % lo, align_bytes=64)
            nc.vector.quantize_mx(
                out=z_codes[:].bitcast(FP8X4), scales=z_plane[:], in_=z_bf16[:].rearrange("p c t -> p (c t)")
            )
            z_packed.append((lo, hi, z_codes, z_plane))

        s_banks = [psum.tile([P, N], F32, name="bank%d" % t) for t in range(PACK)]
        s_first = psum.tile([P, N], F32)
        for t in range(PACK):
            cols = slice(t * P, (t + 1) * P)
            for lo, hi, z_codes, z_plane in z_packed:
                bank = s_first if t == 0 and lo == 0 else s_banks[t]
                product(bank[:, lo:hi], c_codes[:, cols], c_plane[:, cols], z_codes[:], z_plane[:])
            if t == 0:
                nc.scalar.activation(window[t][:, :HALF], s_first[:, :HALF], ACT.Copy, scale=SIXTEENTH)
                nc.vector.tensor_scalar_mul(window[t][:, HALF:N], s_banks[t][:, HALF:], SIXTEENTH)
            else:
                nc.scalar.activation(window[t][:, :N], s_banks[t][:], ACT.Copy, scale=SIXTEENTH)

        out_rows = out.rearrange("(a t e) j -> t a e j", t=PACK, e=RUN)
        for t in range(PACK):
            less = keep.tile([P, N], F32, name="less%d" % t)
            gap = keep.tile([P, N], F32, name="gap%d" % t)
            nc.vector.tensor_copy(less[:], window[t][:].indirect(n4_l[:]))
            for lo, hi in HALVES if t == LAST else WHOLE:
                nc.vector.tensor_tensor(
                    gap[:, lo:hi], window[t][:].indirect(entries(n3_l, lo, hi)), less[:, lo:hi], ALU.subtract
                )
                nc.sync.dma_start(out_rows[t, :, :, lo:hi], gap[:, lo:hi])
